import numpy as np
import ml_dtypes


def mxq(x, axis, fmt="e4m3"):
    dtype, down = {"e4m3": (ml_dtypes.float8_e4m3fn, 7), "e5m2": (ml_dtypes.float8_e5m2, 14)}[fmt]
    v = np.moveaxis(np.asarray(x, np.float32).astype(ml_dtypes.bfloat16).astype(np.float64), axis, -1)
    blocks = v.reshape(v.shape[:-1] + (-1, 32))
    amax = np.abs(blocks).max(-1, keepdims=True)
    byte = np.maximum(np.where(amax > 0, np.frexp(amax)[1] - 1 + 127, 0) - down, 1)
    scale = np.exp2(byte - 127.0)
    codes = (blocks / scale).astype(np.float32).astype(dtype).astype(np.float64)
    return np.moveaxis((codes * scale).reshape(v.shape), -1, axis)


WIDE = False


def mx_kscale(k):
    if not WIDE:
        return np.ones(k)
    levels = np.array([10, -10, 5, -5, 0])
    if k % 512:
        return np.exp2(np.random.permutation(np.resize(levels, k // 32))).repeat(32)
    a = np.empty((k // 512, 16))
    for p in range(k // 512):
        a[p, :8] = np.random.permutation(np.resize(levels, 8))
        for g in range(8):
            far = levels[np.abs(levels - a[p, g]) >= 10]
            a[p, g + 8] = far[np.random.randint(len(far))]
    return np.exp2(a.ravel()).repeat(32)


def f64(x):
    return np.asarray(x).astype(np.float64)


def striped(idx):
    return np.tile(idx.reshape(-1, 16).T, (8, 1)).astype(np.uint16)


def unstriped(offs):
    return offs[:16].T.reshape(-1).astype(np.int64)


def striped8(idx):
    return np.concatenate([v.reshape(-1, 16).T for v in idx]).astype(np.uint16)


def unstriped8(offs):
    return np.stack([offs[16 * g:16 * g + 16].T.reshape(-1) for g in range(8)]).astype(np.int64)


E2M1 = np.array([0.0, 0.5, 1.0, 1.5, 2.0, 3.0, 4.0, 6.0, -0.0, -0.5, -1.0, -1.5, -2.0, -3.0, -4.0, -6.0])


def pack_weight(w, fmt):
    k, n = w.shape
    w = f64(np.asarray(w, np.float32).astype(ml_dtypes.bfloat16)).reshape(k // 32, 32, n)
    amax = np.abs(w).max(1)
    if fmt == "e4m3":
        byte = np.frexp(amax)[1] - 1 + 127 - 7
    else:
        mant, ex = np.frexp(amax / 6.0)
        byte = np.where(mant > 0.5, ex, ex - 1) + 127
    byte = np.clip(np.where(amax > 0, byte, 1), 1, 254)
    scaled = (w * np.exp2(127.0 - byte)[:, None, :]).reshape(k, n).astype(np.float32)
    by_word = np.ascontiguousarray(scaled.reshape(k // 512, 128, 4, n).transpose(0, 1, 3, 2))
    if fmt == "e4m3":
        words = by_word.astype(ml_dtypes.float8_e4m3fn).view(np.uint8)
    else:
        c = by_word.astype(ml_dtypes.float4_e2m1fn).view(np.uint8) & 0xF
        words = (c[..., 0::2] | (c[..., 1::2] << 4)).reshape(k // 512, 128, 2 * n)
    return np.ascontiguousarray(words), np.ascontiguousarray(byte.astype(np.uint8).reshape(k // 512, 16, n))


def unpack_weight(words, scales, fmt):
    g, _, n = scales.shape
    words = np.ascontiguousarray(words).reshape(g, 128, n, -1)
    if fmt == "e4m3":
        vals = words.view(ml_dtypes.float8_e4m3fn).astype(np.float64)
    else:
        nib = np.empty((g, 128, n, 4), np.uint8)
        nib[..., 0::2] = words & 0xF
        nib[..., 1::2] = words >> 4
        vals = E2M1[nib]
    vals = vals * np.repeat(np.exp2(scales.astype(np.float64) - 127.0), 8, axis=1)[..., None]
    return vals.transpose(0, 1, 3, 2).reshape(g * 512, n)


def pack_table(v):
    words, scales = pack_weight(v, "e4m3")
    return np.concatenate([words.reshape(words.shape[0], -1), scales.reshape(scales.shape[0], -1)], axis=1)


def unpack_table(tab):
    g, t = tab.shape[0], tab.shape[1] // 528
    return unpack_weight(tab[:, :512 * t].reshape(g, 128, t, 4), tab[:, 512 * t:].reshape(g, 16, t), "e4m3")


K, L, M, T, S = 512, 1536, 1024, 1024, 512


def setup_inputs():
    n = np.random.standard_normal
    s1 = mx_kscale(K)[:, None]
    s2 = mx_kscale(L)[:, None]
    p_w4 = pack_weight(n((K, M)) / np.sqrt(K) / s1, "e2m1")
    return {
        "xT": (n((K, T)) * s1).astype(np.float32),
        "w4_words": p_w4[0],
        "w4_scales": p_w4[1],
        "tab": pack_table(n((L, T)) * s2),
        "u": (n((L, M)) / np.sqrt(L) / s2).astype(np.float32),
        "wgt": np.repeat(np.random.uniform(0.5, 2.0, (8, S)), 16, axis=0).astype(np.float32),
        "b": (0.3 * n(1024)).astype(np.float32),
        "offs": striped(np.random.permutation(T)[:S]),
        "offs2": striped8(np.stack([np.random.permutation(T)[:S] for _ in range(8)])),
    }


def reference(xT, w4_words, w4_scales, tab, u, wgt, b, offs, offs2):
    idx2 = unstriped8(offs2)
    group = np.arange(K) % 512 // 64
    xg = f64(wgt)[np.arange(K) // 4 % 128] * f64(xT)[np.arange(K)[:, None], idx2[group]]
    xT_ = mxq(xg, 0, "e4m3")
    w4_ = unpack_weight(w4_words, w4_scales, "e2m1")
    tab_ = unpack_table(tab)[:, unstriped(offs)]
    u_ = mxq(f64(u), 0, "e4m3")
    y = xT_.T @ w4_ + tab_.T @ u_
    return y + f64(b)[None, :]

@@ -1,0 +1,244 @@
+from contextlib import ExitStack
+
+import concourse.mybir as mybir
+from concourse.masks import make_identity
+
+K, L, M, T, S = 512, 1536, 1024, 1024, 512
+FLOPS = 2 * S * M * (K + L)
+
+F32 = mybir.dt.float32
+BF16 = mybir.dt.bfloat16
+I32 = mybir.dt.int32
+U32 = mybir.dt.uint32
+U16 = mybir.dt.uint16
+U8 = mybir.dt.uint8
+FP8X4 = mybir.dt.float8_e4m3fn_x4
+FP4X4 = mybir.dt.float4_e2m1fn_x4
+MULT = mybir.AluOpType.mult
+ADD = mybir.AluOpType.add
+
+P = 128
+PACK = 4
+PASSES = L // (P * PACK)
+BANK = 512
+HALF = M // 2
+QUARTER = M // 4
+J_TILES = S // P
+
+
+def tile_list_htab_tm_bias_kernel(tc, xT, w4_words, w4_scales, tab, u, wgt, b, offs, offs2, out):
+    nc = tc.nc
+    with ExitStack() as ctx:
+        sb = ctx.enter_context(tc.tile_pool(name="sb", bufs=1))
+        ps = ctx.enter_context(tc.psum_pool(name="ps", bufs=1))
+
+        tab_list = sb.tile([P, S // 16], U16, name="tab_list")
+        head_lists = sb.tile([P, S // 16], U16, name="head_lists")
+        tab_words = [sb.tile([P, T], I32, name="tab_words%d" % a) for a in range(PASSES)]
+        tab_scales = sb.tile([P, T], U8, name="tab_scales", align_bytes=64)
+        w4_codes = sb.tile([P, 2 * M], U8, name="w4_codes", align_bytes=64)
+        w4_plane = sb.tile([P, M], U8, name="w4_plane", align_bytes=64)
+        x_planes = [sb.tile([P, T], F32, name="x_plane%d" % i) for i in range(PACK)]
+        weights = sb.tile([P, S], F32, name="weights")
+        b_rows = sb.tile([P, 2, PACK], F32, name="b_rows")
+        identity = sb.tile([P, P], F32, name="identity")
+        bias = sb.tile([P, M], F32, name="bias")
+        picked = sb.tile([P, PACK, S], F32, name="picked")
+        xg_bf = sb.tile([P, S, PACK], BF16, name="xg_bf", align_bytes=64)
+        xg_codes = sb.tile([P, S], U32, name="xg_codes", align_bytes=64)
+        xg_plane = sb.tile([P, S], U8, name="xg_plane", align_bytes=64)
+        v_codes = [sb.tile([P, S], U32, name="v_codes%d" % a, align_bytes=64) for a in range(PASSES)]
+        v_planes = sb.tile([P, S], U8, name="v_planes", align_bytes=64)
+
+        nc.vector.memset(tab_scales[:].bitcast(I32), 0)
+        nc.vector.memset(w4_plane[:].bitcast(I32), 0)
+
+        def load_tab(a):
+            words = tab[a, 0 : PACK * P * T].rearrange("(p x) -> p x", p=P)
+            nc.sync.dma_start(tab_words[a][:], words.bitcast(I32))
+
+        def load_x(i):
+            nc.sync.dma_start(x_planes[i][:], xT.rearrange("(p i) t -> p i t", i=PACK)[:, i, :])
+
+        u_raw, u_bf, u_codes, u_plane = {}, {}, {}, {}
+
+        def load_u(a, c0, w):
+            u_raw[a, c0] = sb.tile([P, PACK, w], F32, name="u_raw%d_%d" % (a, c0))
+            rows = u[a * P * PACK : (a + 1) * P * PACK, c0 : c0 + w]
+            nc.sync.dma_start(u_raw[a, c0][:], rows.rearrange("(p i) n -> p i n", i=PACK))
+
+        def interleave(copy, dst, src):
+            copy(dst.rearrange("p (c e) i -> p c i e", e=4), src.rearrange("p i (c e) -> p c i e", e=4))
+
+        def round_u(a, c0, w, on_vector=0):
+            u_bf[a, c0] = sb.tile([P, w, PACK], BF16, name="u_bf%d_%d" % (a, c0), align_bytes=64)
+            cut = w - on_vector
+            if cut > 0:
+                interleave(nc.scalar.copy, u_bf[a, c0][:, 0:cut, :], u_raw[a, c0][:, :, 0:cut])
+            if cut < w:
+                interleave(nc.vector.tensor_copy, u_bf[a, c0][:, cut:w, :], u_raw[a, c0][:, :, cut:w])
+
+        def quantize_u(a, c0, w):
+            u_codes[a, c0] = sb.tile([P, w], U32, name="u_codes%d_%d" % (a, c0), align_bytes=64)
+            u_plane[a, c0] = sb.tile([P, w], U8, name="u_plane%d_%d" % (a, c0), align_bytes=64)
+            nc.vector.quantize_mx(
+                out=u_codes[a, c0][:].bitcast(FP8X4),
+                scales=u_plane[a, c0][:],
+                in_=u_bf[a, c0][:].rearrange("p n i -> p (n i)"),
+            )
+
+        def gather_tab(a):
+            nc.vector.tensor_copy(v_codes[a][:], tab_words[a][:].bitcast(U32).indirect(tab_list[:]))
+
+        def gather_x(i):
+            nc.vector.tensor_tensor(picked[:, i, :], x_planes[i][:].indirect(head_lists[:]), weights[:], MULT)
+
+        def table_pass(acc, jt, a, piece, n0, w, start=False, stop=False):
+            js = slice(jt * P, (jt + 1) * P)
+            ns = slice(n0 - piece, n0 - piece + w)
+            nc.tensor.matmul_mx(
+                out=acc,
+                lhsT=v_codes[a][:, js].bitcast(FP8X4),
+                lhsT_scale=v_planes[4 * a : P, js],
+                rhs=u_codes[a, piece][:, ns].bitcast(FP8X4),
+                rhs_scale=u_plane[a, piece][:, ns],
+                start=start,
+                stop=stop,
+            )
+
+        def heads_pass(acc, jt, n0, w, start=False):
+            js = slice(jt * P, (jt + 1) * P)
+            nc.tensor.matmul_mx(
+                out=acc,
+                lhsT=xg_codes[:, js].bitcast(FP8X4),
+                lhsT_scale=xg_plane[:, js],
+                rhs=w4_codes[:, 2 * n0 : 2 * (n0 + w)].bitcast(FP4X4),
+                rhs_scale=w4_plane[:, n0 : n0 + w],
+                start=start,
+                stop=False,
+            )
+
+        def load_tab_scales(a0, a1):
+            for q in range(4):
+                first = PACK * P * T + 4 * q * T
+                rows = tab[a0:a1, first : first + 4 * T].rearrange("a (r t) -> a r t", r=4)
+                nc.sync.dma_start(tab_scales[32 * q + 4 * a0 : 32 * q + 4 * a1, :].bitcast(I32), rows.bitcast(I32))
+
+        def load_w4_scales():
+            for q in range(4):
+                nc.sync.dma_start(w4_plane[32 * q : 32 * q + 4, :].bitcast(I32), w4_scales[0, 4 * q : 4 * q + 4, :].bitcast(I32))
+
+        nc.scalar.dma_start(b_rows[:], b.rearrange("(h p c) -> p h c", h=2, c=PACK))
+        nc.sync.dma_start(head_lists[:], offs2)
+        load_x(0)
+        nc.sync.dma_start(tab_list[:], offs)
+        nc.sync.dma_start(weights[:], wgt)
+        load_x(1)
+        load_x(2)
+        load_tab_scales(0, 2)
+        load_u(0, 0, HALF)
+        load_x(3)
+        load_tab(0)
+        load_tab_scales(2, 3)
+        nc.sync.dma_start(w4_codes[:].bitcast(I32), w4_words[0].bitcast(I32))
+        load_u(1, 0, HALF)
+        load_tab(1)
+        load_w4_scales()
+        load_tab(2)
+        load_u(2, 0, HALF)
+        load_u(0, HALF, HALF)
+        load_u(1, HALF, HALF)
+        load_u(2, HALF, QUARTER)
+        load_u(2, HALF + QUARTER, QUARTER)
+
+        make_identity(nc, identity[:])
+        for h in range(2):
+            spread = ps.tile([P, PACK, P], F32, name="spread", tag="right%d" % h)
+            for c in range(PACK):
+                nc.tensor.transpose(spread[:, c, :], b_rows[:, h, c : c + 1].to_broadcast([P, P]), identity[:])
+            nc.scalar.copy(
+                bias[:, h * HALF : (h + 1) * HALF].rearrange("q (p c) -> q p c", c=PACK),
+                spread[:].rearrange("q c p -> q p c"),
+            )
+
+        left = [ps.tile([P, BANK], F32, name="left%d" % jt) for jt in range(J_TILES)]
+        right = [ps.tile([P, 2, QUARTER], F32, name="right%d" % r, tag="right%d" % r) for r in range(4)]
+
+        def left_table(a, start=False, stop=False):
+            for jt in range(J_TILES):
+                table_pass(left[jt][:], jt, a, 0, 0, HALF, start, stop)
+
+        def left_heads():
+            for jt in range(J_TILES):
+                heads_pass(left[jt][:], jt, 0, HALF)
+
+        def right_table(a, quarter, piece, start=False, stop=False):
+            for jt in range(J_TILES):
+                acc = right[2 * quarter + jt // 2][:, jt % 2, :]
+                table_pass(acc, jt, a, piece, HALF + quarter * QUARTER, QUARTER, start and jt % 2 == 0, stop and jt % 2 == 1)
+
+        def right_heads(quarter):
+            for jt in range(J_TILES):
+                for s in range(QUARTER // P):
+                    acc = right[2 * quarter + jt // 2][:, jt % 2, s * P : (s + 1) * P]
+                    heads_pass(acc, jt, HALF + quarter * QUARTER + s * P, P, jt % 2 == 0 and s == 0)
+
+        def finish_left():
+            for jt in range(J_TILES):
+                res = sb.tile([P, HALF], F32, name="res_left%d" % jt)
+                nc.vector.tensor_tensor(res[:], left[jt][:], bias[:, 0:HALF], ADD)
+                nc.sync.dma_start(out[jt * P : (jt + 1) * P, 0:HALF], res[:])
+
+        def finish_right(quarter):
+            n0 = HALF + quarter * QUARTER
+            for pair in range(2):
+                res = sb.tile([P, 2, QUARTER], F32, name="res_right%d_%d" % (quarter, pair))
+                row = bias[:, n0 : n0 + QUARTER].unsqueeze(1).to_broadcast([P, 2, QUARTER])
+                nc.vector.tensor_tensor(res[:], right[2 * quarter + pair][:], row, ADD)
+                rows = out[2 * pair * P : 2 * (pair + 1) * P, n0 : n0 + QUARTER]
+                nc.sync.dma_start(rows.rearrange("(s p) n -> p s n", p=P), res[:])
+
+        def heads_operand():
+            interleave(nc.scalar.copy, xg_bf[:], picked[:])
+            nc.vector.quantize_mx(
+                out=xg_codes[:].bitcast(FP8X4), scales=xg_plane[:], in_=xg_bf[:].rearrange("p j i -> p (j i)")
+            )
+
+        gather_tab(0)
+        gather_x(0)
+        gather_x(1)
+        round_u(0, 0, HALF)
+        gather_x(2)
+        gather_x(3)
+        heads_operand()
+        quantize_u(0, 0, HALF)
+        nc.vector.tensor_copy(v_planes[:], tab_scales[:].indirect(tab_list[:]))
+        left_table(0, start=True)
+        round_u(1, 0, HALF)
+        gather_tab(1)
+        left_heads()
+        right_heads(0)
+        right_heads(1)
+        quantize_u(1, 0, HALF)
+        left_table(1)
+        gather_tab(2)
+        round_u(2, 0, HALF, on_vector=320)
+        quantize_u(2, 0, HALF)
+        left_table(2, stop=True)
+        round_u(0, HALF, HALF, on_vector=192)
+        quantize_u(0, HALF, HALF)
+        right_table(0, 0, HALF)
+        right_table(0, 1, HALF)
+        round_u(1, HALF, HALF, on_vector=192)
+        quantize_u(1, HALF, HALF)
+        right_table(1, 0, HALF)
+        right_table(1, 1, HALF)
+        round_u(2, HALF, QUARTER, on_vector=128)
+        quantize_u(2, HALF, QUARTER)
+        right_table(2, 0, HALF, stop=True)
+        round_u(2, HALF + QUARTER, QUARTER, on_vector=160)
+        quantize_u(2, HALF + QUARTER, QUARTER)
+        right_table(2, 1, HALF + QUARTER, stop=True)
+        finish_left()
+        finish_right(0)
+        finish_right(1)

@@ -36,7 +36,7 @@ def tile_list_htab_tm_bias_kernel(tc, xT, w4_words, w4_scales, tab, u, wgt, b, o
         head_lists = sb.tile([P, S // 16], U16, name="head_lists")
         tab_words = [sb.tile([P, T], I32, name="tab_words%d" % a) for a in range(PASSES)]
         tab_scales = sb.tile([P, T], U8, name="tab_scales", align_bytes=64)
-        w4_codes = sb.tile([P, 2 * M], U8, name="w4_codes", align_bytes=64)
+        w4_codes = [sb.tile([P, 2 * HALF], U8, name="w4_codes%d" % h, align_bytes=64) for h in range(2)]
         w4_plane = sb.tile([P, M], U8, name="w4_plane", align_bytes=64)
         x_planes = [sb.tile([P, T], F32, name="x_plane%d" % i) for i in range(PACK)]
         weights = sb.tile([P, S], F32, name="weights")
@@ -60,6 +60,7 @@ def tile_list_htab_tm_bias_kernel(tc, xT, w4_words, w4_scales, tab, u, wgt, b, o
         def load_x(i):
             nc.sync.dma_start(x_planes[i][:], xT.rearrange("(p i) t -> p i t", i=PACK)[:, i, :])
 
+        reuse = {2: "u_bf0_512", 3: "u_bf1_512", 4: "u_bf1_768", 5: "u_bf2_768"}
         u_raw, u_bf, u_codes, u_plane = {}, {}, {}, {}
 
         def load_u(a, c0, w):
@@ -70,8 +71,12 @@ def tile_list_htab_tm_bias_kernel(tc, xT, w4_words, w4_scales, tab, u, wgt, b, o
         def interleave(copy, dst, src):
             copy(dst.rearrange("p (c e) i -> p c i e", e=4), src.rearrange("p i (c e) -> p c i e", e=4))
 
+        def round_pair(a, c0):
+            u_bf[a, c0] = sb.tile([P, HALF, PACK], BF16, name="u_bf%d_%d" % (a, c0), align_bytes=64)
+            return u_bf[a, c0]
+
         def round_u(a, c0, w, on_vector=0):
-            u_bf[a, c0] = sb.tile([P, w, PACK], BF16, name="u_bf%d_%d" % (a, c0), align_bytes=64)
+            u_bf[a, c0] = sb.tile([P, w, PACK], BF16, name="u_bf%d_%d" % (a, c0), tag="u_bf%d_%d" % (a, c0), align_bytes=64)
             cut = w - on_vector
             if cut > 0:
                 interleave(nc.scalar.copy, u_bf[a, c0][:, 0:cut, :], u_raw[a, c0][:, :, 0:cut])
@@ -112,7 +117,7 @@ def tile_list_htab_tm_bias_kernel(tc, xT, w4_words, w4_scales, tab, u, wgt, b, o
                 out=acc,
                 lhsT=xg_codes[:, js].bitcast(FP8X4),
                 lhsT_scale=xg_plane[:, js],
-                rhs=w4_codes[:, 2 * n0 : 2 * (n0 + w)].bitcast(FP4X4),
+                rhs=w4_codes[n0 // HALF][:, 2 * (n0 % HALF) : 2 * (n0 % HALF + w)].bitcast(FP4X4),
                 rhs_scale=w4_plane[:, n0 : n0 + w],
                 start=start,
                 stop=False,
@@ -128,27 +133,33 @@ def tile_list_htab_tm_bias_kernel(tc, xT, w4_words, w4_scales, tab, u, wgt, b, o
             for q in range(4):
                 nc.sync.dma_start(w4_plane[32 * q : 32 * q + 4, :].bitcast(I32), w4_scales[0, 4 * q : 4 * q + 4, :].bitcast(I32))
 
+        def load_w4(h):
+            cols = slice(2 * h * HALF, 2 * (h + 1) * HALF)
+            nc.sync.dma_start(w4_codes[h][:].bitcast(I32), w4_words[0][:, cols].bitcast(I32))
+
         nc.scalar.dma_start(b_rows[:], b.rearrange("(h p c) -> p h c", h=2, c=PACK))
         nc.sync.dma_start(head_lists[:], offs2)
         load_x(0)
-        nc.sync.dma_start(tab_list[:], offs)
         nc.sync.dma_start(weights[:], wgt)
+        nc.sync.dma_start(tab_list[:], offs)
         load_x(1)
         load_x(2)
         load_tab_scales(0, 2)
         load_u(0, 0, HALF)
         load_x(3)
-        load_tab(0)
         load_tab_scales(2, 3)
-        nc.sync.dma_start(w4_codes[:].bitcast(I32), w4_words[0].bitcast(I32))
+        load_tab(0)
         load_u(1, 0, HALF)
+        load_w4(0)
         load_tab(1)
         load_w4_scales()
         load_tab(2)
         load_u(2, 0, HALF)
         load_u(0, HALF, HALF)
-        load_u(1, HALF, HALF)
+        load_w4(1)
+        load_u(1, HALF, QUARTER)
         load_u(2, HALF, QUARTER)
+        load_u(1, HALF + QUARTER, QUARTER)
         load_u(2, HALF + QUARTER, QUARTER)
 
         make_identity(nc, identity[:])
@@ -185,14 +196,14 @@ def tile_list_htab_tm_bias_kernel(tc, xT, w4_words, w4_scales, tab, u, wgt, b, o
 
         def finish_left():
             for jt in range(J_TILES):
-                res = sb.tile([P, HALF], F32, name="res_left%d" % jt)
+                res = sb.tile([P, HALF], F32, name="res_left%d" % jt, tag=reuse.get(jt, "res_left%d" % jt), align_bytes=64)
                 nc.vector.tensor_tensor(res[:], left[jt][:], bias[:, 0:HALF], ADD)
                 nc.sync.dma_start(out[jt * P : (jt + 1) * P, 0:HALF], res[:])
 
         def finish_right(quarter):
             n0 = HALF + quarter * QUARTER
             for pair in range(2):
-                res = sb.tile([P, 2, QUARTER], F32, name="res_right%d_%d" % (quarter, pair))
+                res = sb.tile([P, 2, QUARTER], F32, name="res_right%d_%d" % (quarter, pair), tag=reuse.get(4 + 2 * quarter + pair, "res_right%d_%d" % (quarter, pair)), align_bytes=64)
                 row = bias[:, n0 : n0 + QUARTER].unsqueeze(1).to_broadcast([P, 2, QUARTER])
                 nc.vector.tensor_tensor(res[:], right[2 * quarter + pair][:], row, ADD)
                 rows = out[2 * pair * P : 2 * (pair + 1) * P, n0 : n0 + QUARTER]
@@ -204,38 +215,40 @@ def tile_list_htab_tm_bias_kernel(tc, xT, w4_words, w4_scales, tab, u, wgt, b, o
                 out=xg_codes[:].bitcast(FP8X4), scales=xg_plane[:], in_=xg_bf[:].rearrange("p j i -> p (j i)")
             )
 
-        gather_tab(0)
         gather_x(0)
         gather_x(1)
         round_u(0, 0, HALF)
         gather_x(2)
         gather_x(3)
         heads_operand()
-        quantize_u(0, 0, HALF)
+        gather_tab(0)
         nc.vector.tensor_copy(v_planes[:], tab_scales[:].indirect(tab_list[:]))
+        quantize_u(0, 0, HALF)
         left_table(0, start=True)
-        round_u(1, 0, HALF)
         gather_tab(1)
-        left_heads()
-        right_heads(0)
-        right_heads(1)
+        round_u(1, 0, HALF)
         quantize_u(1, 0, HALF)
         left_table(1)
+        left_heads()
         gather_tab(2)
         round_u(2, 0, HALF, on_vector=320)
         quantize_u(2, 0, HALF)
         left_table(2, stop=True)
+        right_heads(0)
+        right_heads(1)
         round_u(0, HALF, HALF, on_vector=192)
         quantize_u(0, HALF, HALF)
         right_table(0, 0, HALF)
         right_table(0, 1, HALF)
-        round_u(1, HALF, HALF, on_vector=192)
-        quantize_u(1, HALF, HALF)
+        round_u(1, HALF, QUARTER)
+        quantize_u(1, HALF, QUARTER)
         right_table(1, 0, HALF)
-        right_table(1, 1, HALF)
-        round_u(2, HALF, QUARTER, on_vector=128)
+        round_u(2, HALF, QUARTER)
         quantize_u(2, HALF, QUARTER)
         right_table(2, 0, HALF, stop=True)
+        round_u(1, HALF + QUARTER, QUARTER)
+        quantize_u(1, HALF + QUARTER, QUARTER)
+        right_table(1, 1, HALF + QUARTER)
         round_u(2, HALF + QUARTER, QUARTER, on_vector=160)
         quantize_u(2, HALF + QUARTER, QUARTER)
         right_table(2, 1, HALF + QUARTER, stop=True)

@@ -36,7 +36,7 @@ def tile_list_htab_tm_bias_kernel(tc, xT, w4_words, w4_scales, tab, u, wgt, b, o
         head_lists = sb.tile([P, S // 16], U16, name="head_lists")
         tab_words = [sb.tile([P, T], I32, name="tab_words%d" % a) for a in range(PASSES)]
         tab_scales = sb.tile([P, T], U8, name="tab_scales", align_bytes=64)
-        w4_codes = [sb.tile([P, 2 * HALF], U8, name="w4_codes%d" % h, align_bytes=64) for h in range(2)]
+        w4_codes = sb.tile([P, 2 * M], U8, name="w4_codes", align_bytes=64)
         w4_plane = sb.tile([P, M], U8, name="w4_plane", align_bytes=64)
         x_planes = [sb.tile([P, T], F32, name="x_plane%d" % i) for i in range(PACK)]
         weights = sb.tile([P, S], F32, name="weights")
@@ -60,7 +60,7 @@ def tile_list_htab_tm_bias_kernel(tc, xT, w4_words, w4_scales, tab, u, wgt, b, o
         def load_x(i):
             nc.sync.dma_start(x_planes[i][:], xT.rearrange("(p i) t -> p i t", i=PACK)[:, i, :])
 
-        reuse = {2: "u_bf0_512", 3: "u_bf1_512", 4: "u_bf1_768", 5: "u_bf2_768"}
+        reuse = {4: "u_bf1_768", 5: "u_bf2_768"}
         u_raw, u_bf, u_codes, u_plane = {}, {}, {}, {}
 
         def load_u(a, c0, w):
@@ -117,7 +117,7 @@ def tile_list_htab_tm_bias_kernel(tc, xT, w4_words, w4_scales, tab, u, wgt, b, o
                 out=acc,
                 lhsT=xg_codes[:, js].bitcast(FP8X4),
                 lhsT_scale=xg_plane[:, js],
-                rhs=w4_codes[n0 // HALF][:, 2 * (n0 % HALF) : 2 * (n0 % HALF + w)].bitcast(FP4X4),
+                rhs=w4_codes[:, 2 * n0 : 2 * (n0 + w)].bitcast(FP4X4),
                 rhs_scale=w4_plane[:, n0 : n0 + w],
                 start=start,
                 stop=False,
@@ -127,11 +127,11 @@ def tile_list_htab_tm_bias_kernel(tc, xT, w4_words, w4_scales, tab, u, wgt, b, o
             for q in range(4):
                 first = PACK * P * T + 4 * q * T
                 rows = tab[a0:a1, first : first + 4 * T].rearrange("a (r t) -> a r t", r=4)
-                nc.sync.dma_start(tab_scales[32 * q + 4 * a0 : 32 * q + 4 * a1, :].bitcast(I32), rows.bitcast(I32))
+                nc.gpsimd.dma_start(tab_scales[32 * q + 4 * a0 : 32 * q + 4 * a1, :].bitcast(I32), rows.bitcast(I32))
 
         def load_w4_scales():
             for q in range(4):
-                nc.sync.dma_start(w4_plane[32 * q : 32 * q + 4, :].bitcast(I32), w4_scales[0, 4 * q : 4 * q + 4, :].bitcast(I32))
+                nc.gpsimd.dma_start(w4_plane[32 * q : 32 * q + 4, :].bitcast(I32), w4_scales[0, 4 * q : 4 * q + 4, :].bitcast(I32))
 
         def load_w4(h):
             cols = slice(2 * h * HALF, 2 * (h + 1) * HALF)
@@ -144,23 +144,21 @@ def tile_list_htab_tm_bias_kernel(tc, xT, w4_words, w4_scales, tab, u, wgt, b, o
         nc.sync.dma_start(tab_list[:], offs)
         load_x(1)
         load_x(2)
-        load_tab_scales(0, 2)
         load_u(0, 0, HALF)
         load_x(3)
-        load_tab_scales(2, 3)
         load_tab(0)
         load_u(1, 0, HALF)
-        load_w4(0)
+        nc.sync.dma_start(w4_codes[:].bitcast(I32), w4_words[0].bitcast(I32))
         load_tab(1)
-        load_w4_scales()
         load_tab(2)
         load_u(2, 0, HALF)
         load_u(0, HALF, HALF)
-        load_w4(1)
         load_u(1, HALF, QUARTER)
         load_u(2, HALF, QUARTER)
         load_u(1, HALF + QUARTER, QUARTER)
         load_u(2, HALF + QUARTER, QUARTER)
+        load_tab_scales(0, PASSES)
+        load_w4_scales()
 
         make_identity(nc, identity[:])
         for h in range(2):
@@ -231,12 +229,12 @@ def tile_list_htab_tm_bias_kernel(tc, xT, w4_words, w4_scales, tab, u, wgt, b, o
         left_table(1)
         left_heads()
         gather_tab(2)
-        round_u(2, 0, HALF, on_vector=320)
+        round_u(2, 0, HALF, on_vector=256)
         quantize_u(2, 0, HALF)
         left_table(2, stop=True)
         right_heads(0)
         right_heads(1)
-        round_u(0, HALF, HALF, on_vector=192)
+        round_u(0, HALF, HALF, on_vector=256)
         quantize_u(0, HALF, HALF)
         right_table(0, 0, HALF)
         right_table(0, 1, HALF)

from contextlib import ExitStack

import concourse.mybir as mybir
from concourse.masks import make_identity

K, L, M, T, S = 512, 1536, 1024, 1024, 512
FLOPS = 2 * S * M * (K + L)

F32 = mybir.dt.float32
BF16 = mybir.dt.bfloat16
I32 = mybir.dt.int32
U32 = mybir.dt.uint32
U16 = mybir.dt.uint16
U8 = mybir.dt.uint8
FP8X4 = mybir.dt.float8_e4m3fn_x4
FP4X4 = mybir.dt.float4_e2m1fn_x4
MULT = mybir.AluOpType.mult
ADD = mybir.AluOpType.add

P = 128
PACK = 4
PASSES = L // (P * PACK)
BANK = 512
HALF = M // 2
QUARTER = M // 4
J_TILES = S // P


def tile_list_htab_tm_bias_kernel(tc, xT, w4_words, w4_scales, tab, u, wgt, b, offs, offs2, out):
    nc = tc.nc
    with ExitStack() as ctx:
        sb = ctx.enter_context(tc.tile_pool(name="sb", bufs=1))
        ps = ctx.enter_context(tc.psum_pool(name="ps", bufs=1))

        tab_list = sb.tile([P, S // 16], U16, name="tab_list")
        head_lists = sb.tile([P, S // 16], U16, name="head_lists")
        tab_words = [sb.tile([P, T], I32, name="tab_words%d" % a) for a in range(PASSES)]
        tab_scales = sb.tile([P, T], U8, name="tab_scales", align_bytes=64)
        w4_codes = sb.tile([P, 2 * M], U8, name="w4_codes", align_bytes=64)
        w4_plane = sb.tile([P, M], U8, name="w4_plane", align_bytes=64)
        x_planes = [sb.tile([P, T], F32, name="x_plane%d" % i) for i in range(PACK)]
        weights = sb.tile([P, S], F32, name="weights")
        b_rows = sb.tile([P, 2, PACK], F32, name="b_rows")
        identity = sb.tile([P, P], F32, name="identity")
        bias = sb.tile([P, M], F32, name="bias")
        picked = sb.tile([P, PACK, S], F32, name="picked")
        xg_bf = sb.tile([P, S, PACK], BF16, name="xg_bf", align_bytes=64)
        xg_codes = sb.tile([P, S], U32, name="xg_codes", align_bytes=64)
        xg_plane = sb.tile([P, S], U8, name="xg_plane", align_bytes=64)
        v_codes = [sb.tile([P, S], U32, name="v_codes%d" % a, align_bytes=64) for a in range(PASSES)]
        v_planes = sb.tile([P, S], U8, name="v_planes", align_bytes=64)

        nc.vector.memset(tab_scales[:].bitcast(I32), 0)
        nc.vector.memset(w4_plane[:].bitcast(I32), 0)

        def load_tab(a):
            words = tab[a, 0 : PACK * P * T].rearrange("(p x) -> p x", p=P)
            nc.sync.dma_start(tab_words[a][:], words.bitcast(I32))

        def load_x(i):
            nc.sync.dma_start(x_planes[i][:], xT.rearrange("(p i) t -> p i t", i=PACK)[:, i, :])

        reuse = {4: "u_bf1_768", 5: "u_bf2_768"}
        u_raw, u_bf, u_codes, u_plane = {}, {}, {}, {}

        def load_u(a, c0, w):
            u_raw[a, c0] = sb.tile([P, PACK, w], F32, name="u_raw%d_%d" % (a, c0))
            rows = u[a * P * PACK : (a + 1) * P * PACK, c0 : c0 + w]
            nc.sync.dma_start(u_raw[a, c0][:], rows.rearrange("(p i) n -> p i n", i=PACK))

        def interleave(copy, dst, src):
            copy(dst.rearrange("p (c e) i -> p c i e", e=4), src.rearrange("p i (c e) -> p c i e", e=4))

        def round_pair(a, c0):
            u_bf[a, c0] = sb.tile([P, HALF, PACK], BF16, name="u_bf%d_%d" % (a, c0), align_bytes=64)
            return u_bf[a, c0]

        def round_u(a, c0, w, on_vector=0):
            u_bf[a, c0] = sb.tile([P, w, PACK], BF16, name="u_bf%d_%d" % (a, c0), tag="u_bf%d_%d" % (a, c0), align_bytes=64)
            cut = w - on_vector
            if cut > 0:
                interleave(nc.scalar.copy, u_bf[a, c0][:, 0:cut, :], u_raw[a, c0][:, :, 0:cut])
            if cut < w:
                interleave(nc.vector.tensor_copy, u_bf[a, c0][:, cut:w, :], u_raw[a, c0][:, :, cut:w])

        def quantize_u(a, c0, w):
            u_codes[a, c0] = sb.tile([P, w], U32, name="u_codes%d_%d" % (a, c0), align_bytes=64)
            u_plane[a, c0] = sb.tile([P, w], U8, name="u_plane%d_%d" % (a, c0), align_bytes=64)
            nc.vector.quantize_mx(
                out=u_codes[a, c0][:].bitcast(FP8X4),
                scales=u_plane[a, c0][:],
                in_=u_bf[a, c0][:].rearrange("p n i -> p (n i)"),
            )

        def gather_tab(a):
            nc.vector.tensor_copy(v_codes[a][:], tab_words[a][:].bitcast(U32).indirect(tab_list[:]))

        def gather_x(i):
            nc.vector.tensor_tensor(picked[:, i, :], x_planes[i][:].indirect(head_lists[:]), weights[:], MULT)

        def table_pass(acc, jt, a, piece, n0, w, start=False, stop=False):
            js = slice(jt * P, (jt + 1) * P)
            ns = slice(n0 - piece, n0 - piece + w)
            nc.tensor.matmul_mx(
                out=acc,
                lhsT=v_codes[a][:, js].bitcast(FP8X4),
                lhsT_scale=v_planes[4 * a : P, js],
                rhs=u_codes[a, piece][:, ns].bitcast(FP8X4),
                rhs_scale=u_plane[a, piece][:, ns],
                start=start,
                stop=stop,
            )

        def heads_pass(acc, jt, n0, w, start=False):
            js = slice(jt * P, (jt + 1) * P)
            nc.tensor.matmul_mx(
                out=acc,
                lhsT=xg_codes[:, js].bitcast(FP8X4),
                lhsT_scale=xg_plane[:, js],
                rhs=w4_codes[:, 2 * n0 : 2 * (n0 + w)].bitcast(FP4X4),
                rhs_scale=w4_plane[:, n0 : n0 + w],
                start=start,
                stop=False,
            )

        def load_tab_scales(a0, a1):
            for q in range(4):
                first = PACK * P * T + 4 * q * T
                rows = tab[a0:a1, first : first + 4 * T].rearrange("a (r t) -> a r t", r=4)
                nc.gpsimd.dma_start(tab_scales[32 * q + 4 * a0 : 32 * q + 4 * a1, :].bitcast(I32), rows.bitcast(I32))

        def load_w4_scales():
            for q in range(4):
                nc.gpsimd.dma_start(w4_plane[32 * q : 32 * q + 4, :].bitcast(I32), w4_scales[0, 4 * q : 4 * q + 4, :].bitcast(I32))

        def load_w4(h):
            cols = slice(2 * h * HALF, 2 * (h + 1) * HALF)
            nc.sync.dma_start(w4_codes[h][:].bitcast(I32), w4_words[0][:, cols].bitcast(I32))

        nc.scalar.dma_start(b_rows[:], b.rearrange("(h p c) -> p h c", h=2, c=PACK))
        nc.sync.dma_start(head_lists[:], offs2)
        load_x(0)
        nc.sync.dma_start(weights[:], wgt)
        nc.sync.dma_start(tab_list[:], offs)
        load_x(1)
        load_x(2)
        load_u(0, 0, HALF)
        load_x(3)
        load_tab(0)
        load_u(1, 0, HALF)
        nc.sync.dma_start(w4_codes[:].bitcast(I32), w4_words[0].bitcast(I32))
        load_tab(1)
        load_tab(2)
        load_u(2, 0, HALF)
        load_u(0, HALF, HALF)
        load_u(1, HALF, QUARTER)
        load_u(2, HALF, QUARTER)
        load_u(1, HALF + QUARTER, QUARTER)
        load_u(2, HALF + QUARTER, QUARTER)
        load_tab_scales(0, PASSES)
        load_w4_scales()

        make_identity(nc, identity[:])
        for h in range(2):
            spread = ps.tile([P, PACK, P], F32, name="spread", tag="right%d" % h)
            for c in range(PACK):
                nc.tensor.transpose(spread[:, c, :], b_rows[:, h, c : c + 1].to_broadcast([P, P]), identity[:])
            nc.scalar.copy(
                bias[:, h * HALF : (h + 1) * HALF].rearrange("q (p c) -> q p c", c=PACK),
                spread[:].rearrange("q c p -> q p c"),
            )

        left = [ps.tile([P, BANK], F32, name="left%d" % jt) for jt in range(J_TILES)]
        right = [ps.tile([P, 2, QUARTER], F32, name="right%d" % r, tag="right%d" % r) for r in range(4)]

        def left_table(a, start=False, stop=False):
            for jt in range(J_TILES):
                table_pass(left[jt][:], jt, a, 0, 0, HALF, start, stop)

        def left_heads():
            for jt in range(J_TILES):
                heads_pass(left[jt][:], jt, 0, HALF)

        def right_table(a, quarter, piece, start=False, stop=False):
            for jt in range(J_TILES):
                acc = right[2 * quarter + jt // 2][:, jt % 2, :]
                table_pass(acc, jt, a, piece, HALF + quarter * QUARTER, QUARTER, start and jt % 2 == 0, stop and jt % 2 == 1)

        def right_heads(quarter):
            for jt in range(J_TILES):
                for s in range(QUARTER // P):
                    acc = right[2 * quarter + jt // 2][:, jt % 2, s * P : (s + 1) * P]
                    heads_pass(acc, jt, HALF + quarter * QUARTER + s * P, P, jt % 2 == 0 and s == 0)

        def finish_left():
            for jt in range(J_TILES):
                res = sb.tile([P, HALF], F32, name="res_left%d" % jt, tag=reuse.get(jt, "res_left%d" % jt), align_bytes=64)
                nc.vector.tensor_tensor(res[:], left[jt][:], bias[:, 0:HALF], ADD)
                nc.sync.dma_start(out[jt * P : (jt + 1) * P, 0:HALF], res[:])

        def finish_right(quarter):
            n0 = HALF + quarter * QUARTER
            for pair in range(2):
                res = sb.tile([P, 2, QUARTER], F32, name="res_right%d_%d" % (quarter, pair), tag=reuse.get(4 + 2 * quarter + pair, "res_right%d_%d" % (quarter, pair)), align_bytes=64)
                row = bias[:, n0 : n0 + QUARTER].unsqueeze(1).to_broadcast([P, 2, QUARTER])
                nc.vector.tensor_tensor(res[:], right[2 * quarter + pair][:], row, ADD)
                rows = out[2 * pair * P : 2 * (pair + 1) * P, n0 : n0 + QUARTER]
                nc.sync.dma_start(rows.rearrange("(s p) n -> p s n", p=P), res[:])

        def heads_operand():
            interleave(nc.scalar.copy, xg_bf[:], picked[:])
            nc.vector.quantize_mx(
                out=xg_codes[:].bitcast(FP8X4), scales=xg_plane[:], in_=xg_bf[:].rearrange("p j i -> p (j i)")
            )

        gather_x(0)
        gather_x(1)
        round_u(0, 0, HALF)
        gather_x(2)
        gather_x(3)
        heads_operand()
        gather_tab(0)
        nc.vector.tensor_copy(v_planes[:], tab_scales[:].indirect(tab_list[:]))
        quantize_u(0, 0, HALF)
        left_table(0, start=True)
        gather_tab(1)
        round_u(1, 0, HALF)
        quantize_u(1, 0, HALF)
        left_table(1)
        left_heads()
        gather_tab(2)
        round_u(2, 0, HALF, on_vector=256)
        quantize_u(2, 0, HALF)
        left_table(2, stop=True)
        right_heads(0)
        right_heads(1)
        round_u(0, HALF, HALF, on_vector=256)
        quantize_u(0, HALF, HALF)
        right_table(0, 0, HALF)
        right_table(0, 1, HALF)
        round_u(1, HALF, QUARTER)
        quantize_u(1, HALF, QUARTER)
        right_table(1, 0, HALF)
        round_u(2, HALF, QUARTER)
        quantize_u(2, HALF, QUARTER)
        right_table(2, 0, HALF, stop=True)
        round_u(1, HALF + QUARTER, QUARTER)
        quantize_u(1, HALF + QUARTER, QUARTER)
        right_table(1, 1, HALF + QUARTER)
        round_u(2, HALF + QUARTER, QUARTER, on_vector=160)
        quantize_u(2, HALF + QUARTER, QUARTER)
        right_table(2, 1, HALF + QUARTER, stop=True)
        finish_left()
        finish_right(0)
        finish_right(1)
